import numpy as np
import ml_dtypes


def mxq(x, axis, fmt="e4m3"):
    dtype, down = {"e4m3": (ml_dtypes.float8_e4m3fn, 7), "e5m2": (ml_dtypes.float8_e5m2, 14)}[fmt]
    v = np.moveaxis(np.asarray(x, np.float32).astype(ml_dtypes.bfloat16).astype(np.float64), axis, -1)
    blocks = v.reshape(v.shape[:-1] + (-1, 32))
    amax = np.abs(blocks).max(-1, keepdims=True)
    byte = np.maximum(np.where(amax > 0, np.frexp(amax)[1] - 1 + 127, 0) - down, 1)
    scale = np.exp2(byte - 127.0)
    codes = (blocks / scale).astype(np.float32).astype(dtype).astype(np.float64)
    return np.moveaxis((codes * scale).reshape(v.shape), -1, axis)


WIDE = False


def mx_kscale(k):
    if not WIDE:
        return np.ones(k)
    levels = np.array([10, -10, 5, -5, 0])
    if k % 512:
        return np.exp2(np.random.permutation(np.resize(levels, k // 32))).repeat(32)
    a = np.empty((k // 512, 16))
    for p in range(k // 512):
        a[p, :8] = np.random.permutation(np.resize(levels, 8))
        for g in range(8):
            far = levels[np.abs(levels - a[p, g]) >= 10]
            a[p, g + 8] = far[np.random.randint(len(far))]
    return np.exp2(a.ravel()).repeat(32)


def f64(x):
    return np.asarray(x).astype(np.float64)


def striped(idx):
    return np.tile(idx.reshape(-1, 16).T, (8, 1)).astype(np.uint16)


def unstriped(offs):
    return offs[:16].T.reshape(-1).astype(np.int64)


def pack_weight(w):
    k, n = w.shape
    w = f64(np.asarray(w, np.float32).astype(ml_dtypes.bfloat16)).reshape(k // 32, 32, n)
    amax = np.abs(w).max(1)
    byte = np.clip(np.where(amax > 0, np.frexp(amax)[1] - 1 + 127 - 7, 1), 1, 254)
    scaled = (w * np.exp2(127.0 - byte)[:, None, :]).reshape(k, n).astype(np.float32)
    words = np.ascontiguousarray(scaled.reshape(k // 512, 128, 4, n).transpose(0, 1, 3, 2)).astype(ml_dtypes.float8_e4m3fn).view(np.uint8)
    return words, np.ascontiguousarray(byte.astype(np.uint8).reshape(k // 512, 16, n))


def unpack_weight(words, scales):
    g, p, n, _ = words.shape
    vals = np.ascontiguousarray(words).view(ml_dtypes.float8_e4m3fn).astype(np.float64) * np.repeat(np.exp2(scales.astype(np.float64) - 127.0), 8, axis=1)[..., None]
    return vals.transpose(0, 1, 3, 2).reshape(g * 512, n)


K, T, S, D, N = 512, 2048, 1024, 4, 128
P = 2 ** 7


def setup_inputs():
    n = np.random.standard_normal
    s = mx_kscale(K)[:, None]
    packed_xT = pack_weight(n((K, T)) * s)
    return {
        "x_words": packed_xT[0],
        "x_scales": packed_xT[1],
        "w1": (n((K, N)) / np.sqrt(K) / s).astype(np.float32),
        "w2": (n((K, N)) / np.sqrt(K) / s).astype(np.float32),
        "bel": (np.tile(np.random.uniform(0.1, 0.4, S), (P, 1))).astype(np.float32),
        "offs": striped(np.random.permutation(T)[:S]),
    }


def reference(x_words, x_scales, w1, w2, bel, offs):
    xq = unpack_weight(x_words, x_scales)[:, unstriped(offs)]
    yq = mxq(f64(w1), 0, "e4m3").T @ xq
    yb = mxq(f64(w2), 0, "e4m3").T @ xq
    trd = 0.8 * np.tanh(yb)
    qnew = yq + trd
    topb = qnew.reshape(len(qnew), -1, D).max(axis=2)
    exb = np.exp(qnew - np.repeat(topb, D, axis=1))
    costb = topb + np.log(exb.reshape(len(exb), -1, D).sum(axis=2))
    return np.exp(qnew - np.repeat(costb, D, axis=1)) - f64(bel)[:1]

@@ -1,0 +1,153 @@
+from contextlib import ExitStack
+
+import concourse.mybir as mybir
+
+F32 = mybir.dt.float32
+BF16 = mybir.dt.bfloat16
+I32 = mybir.dt.int32
+U32 = mybir.dt.uint32
+U16 = mybir.dt.uint16
+U8 = mybir.dt.uint8
+FP8X4 = mybir.dt.float8_e4m3fn_x4
+ALU = mybir.AluOpType
+ACT = mybir.ActivationFunctionType
+AX = mybir.AxisListType
+
+P = 128
+K, T, S, D, N = 512, 2048, 1024, 4, 128
+PACK = 4
+CHUNKS = 4
+W = S // CHUNKS
+V = W // D
+FLOPS = 2 * 2 * K * N * S
+
+
+def tile_picked_ylmsr_price_p_kernel(tc, x_words, x_scales, w1, w2, bel, offs, out):
+    nc = tc.nc
+    with ExitStack() as ctx:
+        sb = ctx.enter_context(tc.tile_pool(name="sb", bufs=1))
+        ps = ctx.enter_context(tc.psum_pool(name="ps", bufs=1))
+
+        offsets = sb.tile([P, S // 16], U16, name="offsets")
+        scale_win = sb.tile([P, T], U8, name="scale_win", align_bytes=64)
+        word_win = sb.tile([P, T], I32, name="word_win", align_bytes=64)
+        w2_raw = sb.tile([P, PACK, N], F32, name="w2_raw")
+        w1_raw = sb.tile([P, PACK, N], F32, name="w1_raw")
+        beliefs = sb.tile([P, S], F32, name="beliefs")
+
+        nc.vector.memset(scale_win[:].bitcast(I32), 0)
+        nc.sync.dma_start(offsets[:], offs)
+        nc.sync.dma_start(out=w2_raw[:], in_=w2.rearrange("(p j) n -> p j n", j=PACK))
+        scale_rows = x_scales[0].bitcast(I32)
+        for r in range(4):
+            queue = nc.sync if r < 2 else nc.scalar
+            queue.dma_start(out=scale_win[r:P:32, :].bitcast(I32), in_=scale_rows[r:16:4, :])
+        nc.sync.dma_start(out=word_win[:], in_=x_words[0].rearrange("p n t -> p (n t)").bitcast(I32))
+        nc.sync.dma_start(out=w1_raw[:], in_=w1.rearrange("(p j) n -> p j n", j=PACK))
+        nc.sync.dma_start(out=beliefs[:], in_=bel)
+
+        def cast(raw, name, tag):
+            grouped = sb.tile([P, N, PACK], BF16, name=name, tag=tag, align_bytes=64)
+            nc.scalar.copy(out=grouped[:], in_=raw[:].rearrange("p j n -> p n j"))
+            return grouped
+
+        def quantize(grouped, name):
+            codes = sb.tile([P, N], U32, name=name + "_codes", align_bytes=64)
+            scales = sb.tile([P, N], U8, name=name + "_scales", align_bytes=64)
+            nc.vector.quantize_mx(out=codes[:].bitcast(FP8X4), scales=scales[:],
+                                  in_=grouped[:].rearrange("p n j -> p (n j)"))
+            return codes, scales
+
+        def gather_words(c, tag):
+            picked = sb.tile([P, W], U32, name="picked%d" % c, tag=tag, align_bytes=64)
+            lst = offsets[:, c * W // 16:(c + 1) * W // 16]
+            nc.vector.tensor_copy(picked[:], word_win[:].bitcast(U32).indirect(lst))
+            return picked
+
+        def product(weights, picked, c, name):
+            acc = ps.tile([P, W], F32, name=name)
+            nc.tensor.matmul_mx(out=acc[:], lhsT=weights[0][:].bitcast(FP8X4), lhsT_scale=weights[1][:],
+                                rhs=picked[:].bitcast(FP8X4), rhs_scale=picked_scales[:, c * W:(c + 1) * W],
+                                start=True, stop=True)
+            return acc
+
+        w2_bf = cast(w2_raw, "w2_bf", "w2_bf")
+        w1_bf = cast(w1_raw, "w1_bf", "w1_bf")
+        picked_scales = sb.tile([P, S], U8, name="picked_scales", align_bytes=64)
+        nc.vector.tensor_copy(picked_scales[:], scale_win[:].indirect(offsets[:]))
+        w2_mx = quantize(w2_bf, "w2")
+        picked = [gather_words(0, "picked0"), gather_words(1, "picked1")]
+        w1_mx = quantize(w1_bf, "w1")
+        picked.append(gather_words(2, "w1_bf"))
+        picked.append(gather_words(3, "picked3"))
+
+        def tiles(name, width):
+            return [sb.tile([P, width], F32, name="%s%d" % (name, c)) for c in range(CHUNKS)]
+
+        def grp(t):
+            return t[:].rearrange("p (v d) -> p v d", d=D)
+
+        def spread(ap):
+            return ap.unsqueeze(2).to_broadcast([P, V, D])
+
+        trade, q, top2, top, z, e = (tiles("trade", W), tiles("q", W), tiles("top2", 2 * V), tiles("top", V),
+                                     tiles("z", W), tiles("e", W))
+        sum2, sums, prod, rprod, rsum = (tiles("sum2", 2 * V), tiles("sums", V), tiles("prod", V // 2),
+                                         tiles("rprod", V // 2), tiles("rsum", V))
+        price, res = tiles("price", W), tiles("res", W)
+
+        def pairs(t):
+            return t[:].rearrange("p (v d) -> p v d", d=2)
+
+        def halves(t):
+            return t[:].rearrange("p (h v) -> p h v", h=2)
+
+        yq = []
+        for c in range(CHUNKS):
+            yb = product(w2_mx, picked[c], c, "yb%d" % c)
+            nc.scalar.activation(trade[c][:], yb[:], ACT.Tanh)
+            yq.append(product(w1_mx, picked[c], c, "yq%d" % c))
+
+        def f_q(c):
+            nc.vector.scalar_tensor_tensor(out=q[c][:], in0=trade[c][:], scalar=0.8, in1=yq[c][:],
+                                           op0=ALU.mult, op1=ALU.add)
+
+        def f_ma(c):
+            nc.vector.tensor_tensor(out=pairs(top2[c]), in0=grp(q[c])[:, :, 0:2], in1=grp(q[c])[:, :, 2:4], op=ALU.max)
+
+        def f_mb(c):
+            nc.vector.tensor_tensor(out=top[c][:], in0=pairs(top2[c])[:, :, 0], in1=pairs(top2[c])[:, :, 1], op=ALU.max)
+
+        def f_sub(c):
+            nc.vector.tensor_tensor(out=grp(z[c]), in0=grp(q[c]), in1=spread(top[c][:]), op=ALU.subtract)
+            nc.scalar.activation(e[c][:], z[c][:], ACT.Exp)
+
+        def f_sa(c):
+            nc.vector.tensor_tensor(out=pairs(sum2[c]), in0=grp(e[c])[:, :, 0:2], in1=grp(e[c])[:, :, 2:4], op=ALU.add)
+
+        def f_sb(c):
+            nc.vector.tensor_tensor(out=sums[c][:], in0=pairs(sum2[c])[:, :, 0], in1=pairs(sum2[c])[:, :, 1], op=ALU.add)
+
+        def f_prod(c):
+            nc.vector.tensor_tensor(out=prod[c][:], in0=halves(sums[c])[:, 0, :], in1=halves(sums[c])[:, 1, :], op=ALU.mult)
+
+        def f_rec(c):
+            nc.vector.reciprocal(out=rprod[c][:], in_=prod[c][:])
+
+        def f_back(c):
+            nc.vector.tensor_tensor(out=halves(rsum[c]), in0=halves(sums[c])[:, ::-1, :],
+                                    in1=rprod[c][:].unsqueeze(1).to_broadcast([P, 2, V // 2]), op=ALU.mult)
+
+        def f_mul(c):
+            nc.vector.tensor_tensor(out=grp(price[c]), in0=grp(e[c]), in1=spread(rsum[c][:]), op=ALU.mult)
+
+        def f_bel(c):
+            cols = slice(c * W, (c + 1) * W)
+            nc.vector.tensor_tensor(out=res[c][:], in0=price[c][:], in1=beliefs[:, cols], op=ALU.subtract)
+            nc.sync.dma_start(out=out[:, cols], in_=res[c][:])
+
+        stages = [f_q, f_ma, f_mb, f_sub, None, f_sa, f_sb, f_prod, f_rec, f_back, f_mul, f_bel]
+        for step in range(len(stages) + CHUNKS - 1):
+            for c in reversed(range(CHUNKS)):
+                if 0 <= step - c < len(stages) and stages[step - c] is not None:
+                    stages[step - c](c)

@@ -40,10 +40,9 @@ def tile_picked_ylmsr_price_p_kernel(tc, x_words, x_scales, w1, w2, bel, offs, o
         nc.sync.dma_start(out=w2_raw[:], in_=w2.rearrange("(p j) n -> p j n", j=PACK))
         scale_rows = x_scales[0].bitcast(I32)
         for r in range(4):
-            queue = nc.sync if r < 2 else nc.scalar
-            queue.dma_start(out=scale_win[r:P:32, :].bitcast(I32), in_=scale_rows[r:16:4, :])
-        nc.sync.dma_start(out=word_win[:], in_=x_words[0].rearrange("p n t -> p (n t)").bitcast(I32))
+            nc.sync.dma_start(out=scale_win[r:P:32, :].bitcast(I32), in_=scale_rows[r:16:4, :])
         nc.sync.dma_start(out=w1_raw[:], in_=w1.rearrange("(p j) n -> p j n", j=PACK))
+        nc.sync.dma_start(out=word_win[:], in_=x_words[0].rearrange("p n t -> p (n t)").bitcast(I32))
         nc.sync.dma_start(out=beliefs[:], in_=bel)
 
         def cast(raw, name, tag):
@@ -76,10 +75,8 @@ def tile_picked_ylmsr_price_p_kernel(tc, x_words, x_scales, w1, w2, bel, offs, o
         picked_scales = sb.tile([P, S], U8, name="picked_scales", align_bytes=64)
         nc.vector.tensor_copy(picked_scales[:], scale_win[:].indirect(offsets[:]))
         w2_mx = quantize(w2_bf, "w2")
-        picked = [gather_words(0, "picked0"), gather_words(1, "picked1")]
         w1_mx = quantize(w1_bf, "w1")
-        picked.append(gather_words(2, "w1_bf"))
-        picked.append(gather_words(3, "picked3"))
+        picked = [gather_words(c, "picked%d" % c) for c in range(CHUNKS)]
 
         def tiles(name, width):
             return [sb.tile([P, width], F32, name="%s%d" % (name, c)) for c in range(CHUNKS)]

@@ -87,9 +87,9 @@ def tile_picked_ylmsr_price_p_kernel(tc, x_words, x_scales, w1, w2, bel, offs, o
         def spread(ap):
             return ap.unsqueeze(2).to_broadcast([P, V, D])
 
-        trade, q, top2, top, z, e = (tiles("trade", W), tiles("q", W), tiles("top2", 2 * V), tiles("top", V),
+        trade, q, top2, top, z, e = (tiles("trade", W), tiles("q", W), None, tiles("top", V),
                                      tiles("z", W), tiles("e", W))
-        sum2, sums, prod, rprod, rsum = (tiles("sum2", 2 * V), tiles("sums", V), tiles("prod", V // 2),
+        sum2, sums, prod, rprod, rsum = (None, tiles("sums", V), tiles("prod", V // 2),
                                          tiles("rprod", V // 2), tiles("rsum", V))
         price, res = tiles("price", W), tiles("res", W)
 
@@ -109,21 +109,15 @@ def tile_picked_ylmsr_price_p_kernel(tc, x_words, x_scales, w1, w2, bel, offs, o
             nc.vector.scalar_tensor_tensor(out=q[c][:], in0=trade[c][:], scalar=0.8, in1=yq[c][:],
                                            op0=ALU.mult, op1=ALU.add)
 
-        def f_ma(c):
-            nc.vector.tensor_tensor(out=pairs(top2[c]), in0=grp(q[c])[:, :, 0:2], in1=grp(q[c])[:, :, 2:4], op=ALU.max)
-
-        def f_mb(c):
-            nc.vector.tensor_tensor(out=top[c][:], in0=pairs(top2[c])[:, :, 0], in1=pairs(top2[c])[:, :, 1], op=ALU.max)
+        def f_max(c):
+            nc.vector.tensor_reduce(out=top[c][:], in_=grp(q[c]), axis=AX.X, op=ALU.max)
 
         def f_sub(c):
             nc.vector.tensor_tensor(out=grp(z[c]), in0=grp(q[c]), in1=spread(top[c][:]), op=ALU.subtract)
             nc.scalar.activation(e[c][:], z[c][:], ACT.Exp)
 
-        def f_sa(c):
-            nc.vector.tensor_tensor(out=pairs(sum2[c]), in0=grp(e[c])[:, :, 0:2], in1=grp(e[c])[:, :, 2:4], op=ALU.add)
-
-        def f_sb(c):
-            nc.vector.tensor_tensor(out=sums[c][:], in0=pairs(sum2[c])[:, :, 0], in1=pairs(sum2[c])[:, :, 1], op=ALU.add)
+        def f_sum(c):
+            nc.vector.tensor_reduce(out=sums[c][:], in_=grp(e[c]), axis=AX.X, op=ALU.add)
 
         def f_prod(c):
             nc.vector.tensor_tensor(out=prod[c][:], in0=halves(sums[c])[:, 0, :], in1=halves(sums[c])[:, 1, :], op=ALU.mult)
@@ -143,8 +137,9 @@ def tile_picked_ylmsr_price_p_kernel(tc, x_words, x_scales, w1, w2, bel, offs, o
             nc.vector.tensor_tensor(out=res[c][:], in0=price[c][:], in1=beliefs[:, cols], op=ALU.subtract)
             nc.sync.dma_start(out=out[:, cols], in_=res[c][:])
 
-        stages = [f_q, f_ma, f_mb, f_sub, None, f_sa, f_sb, f_prod, f_rec, f_back, f_mul, f_bel]
-        for step in range(len(stages) + CHUNKS - 1):
+        stages = [f_q, f_max, f_sub, None, f_sum, f_prod, f_rec, f_back, f_mul, f_bel]
+        lag = [0, 1, 3, 4]
+        for step in range(len(stages) + lag[-1]):
             for c in reversed(range(CHUNKS)):
-                if 0 <= step - c < len(stages) and stages[step - c] is not None:
-                    stages[step - c](c)
+                if 0 <= step - lag[c] < len(stages) and stages[step - lag[c]] is not None:
+                    stages[step - lag[c]](c)

from contextlib import ExitStack

import concourse.mybir as mybir

F32 = mybir.dt.float32
BF16 = mybir.dt.bfloat16
I32 = mybir.dt.int32
U32 = mybir.dt.uint32
U16 = mybir.dt.uint16
U8 = mybir.dt.uint8
FP8X4 = mybir.dt.float8_e4m3fn_x4
ALU = mybir.AluOpType
ACT = mybir.ActivationFunctionType
AX = mybir.AxisListType

P = 128
K, T, S, D, N = 512, 2048, 1024, 4, 128
PACK = 4
CHUNKS = 4
W = S // CHUNKS
V = W // D
FLOPS = 2 * 2 * K * N * S


def tile_picked_ylmsr_price_p_kernel(tc, x_words, x_scales, w1, w2, bel, offs, out):
    nc = tc.nc
    with ExitStack() as ctx:
        sb = ctx.enter_context(tc.tile_pool(name="sb", bufs=1))
        ps = ctx.enter_context(tc.psum_pool(name="ps", bufs=1))

        offsets = sb.tile([P, S // 16], U16, name="offsets")
        scale_win = sb.tile([P, T], U8, name="scale_win", align_bytes=64)
        word_win = sb.tile([P, T], I32, name="word_win", align_bytes=64)
        w2_raw = sb.tile([P, PACK, N], F32, name="w2_raw")
        w1_raw = sb.tile([P, PACK, N], F32, name="w1_raw")
        beliefs = sb.tile([P, S], F32, name="beliefs")

        nc.vector.memset(scale_win[:].bitcast(I32), 0)
        nc.sync.dma_start(offsets[:], offs)
        nc.sync.dma_start(out=w2_raw[:], in_=w2.rearrange("(p j) n -> p j n", j=PACK))
        scale_rows = x_scales[0].bitcast(I32)
        for r in range(4):
            nc.sync.dma_start(out=scale_win[r:P:32, :].bitcast(I32), in_=scale_rows[r:16:4, :])
        nc.sync.dma_start(out=w1_raw[:], in_=w1.rearrange("(p j) n -> p j n", j=PACK))
        nc.sync.dma_start(out=word_win[:], in_=x_words[0].rearrange("p n t -> p (n t)").bitcast(I32))
        nc.sync.dma_start(out=beliefs[:], in_=bel)

        def cast(raw, name, tag):
            grouped = sb.tile([P, N, PACK], BF16, name=name, tag=tag, align_bytes=64)
            nc.scalar.copy(out=grouped[:], in_=raw[:].rearrange("p j n -> p n j"))
            return grouped

        def quantize(grouped, name):
            codes = sb.tile([P, N], U32, name=name + "_codes", align_bytes=64)
            scales = sb.tile([P, N], U8, name=name + "_scales", align_bytes=64)
            nc.vector.quantize_mx(out=codes[:].bitcast(FP8X4), scales=scales[:],
                                  in_=grouped[:].rearrange("p n j -> p (n j)"))
            return codes, scales

        def gather_words(c, tag):
            picked = sb.tile([P, W], U32, name="picked%d" % c, tag=tag, align_bytes=64)
            lst = offsets[:, c * W // 16:(c + 1) * W // 16]
            nc.vector.tensor_copy(picked[:], word_win[:].bitcast(U32).indirect(lst))
            return picked

        def product(weights, picked, c, name):
            acc = ps.tile([P, W], F32, name=name)
            nc.tensor.matmul_mx(out=acc[:], lhsT=weights[0][:].bitcast(FP8X4), lhsT_scale=weights[1][:],
                                rhs=picked[:].bitcast(FP8X4), rhs_scale=picked_scales[:, c * W:(c + 1) * W],
                                start=True, stop=True)
            return acc

        w2_bf = cast(w2_raw, "w2_bf", "w2_bf")
        w1_bf = cast(w1_raw, "w1_bf", "w1_bf")
        picked_scales = sb.tile([P, S], U8, name="picked_scales", align_bytes=64)
        nc.vector.tensor_copy(picked_scales[:], scale_win[:].indirect(offsets[:]))
        w2_mx = quantize(w2_bf, "w2")
        w1_mx = quantize(w1_bf, "w1")
        picked = [gather_words(c, "picked%d" % c) for c in range(CHUNKS)]

        def tiles(name, width):
            return [sb.tile([P, width], F32, name="%s%d" % (name, c)) for c in range(CHUNKS)]

        def grp(t):
            return t[:].rearrange("p (v d) -> p v d", d=D)

        def spread(ap):
            return ap.unsqueeze(2).to_broadcast([P, V, D])

        trade, q, top2, top, z, e = (tiles("trade", W), tiles("q", W), None, tiles("top", V),
                                     tiles("z", W), tiles("e", W))
        sum2, sums, prod, rprod, rsum = (None, tiles("sums", V), tiles("prod", V // 2),
                                         tiles("rprod", V // 2), tiles("rsum", V))
        price, res = tiles("price", W), tiles("res", W)

        def pairs(t):
            return t[:].rearrange("p (v d) -> p v d", d=2)

        def halves(t):
            return t[:].rearrange("p (h v) -> p h v", h=2)

        yq = []
        for c in range(CHUNKS):
            yb = product(w2_mx, picked[c], c, "yb%d" % c)
            nc.scalar.activation(trade[c][:], yb[:], ACT.Tanh)
            yq.append(product(w1_mx, picked[c], c, "yq%d" % c))

        def f_q(c):
            nc.vector.scalar_tensor_tensor(out=q[c][:], in0=trade[c][:], scalar=0.8, in1=yq[c][:],
                                           op0=ALU.mult, op1=ALU.add)

        def f_max(c):
            nc.vector.tensor_reduce(out=top[c][:], in_=grp(q[c]), axis=AX.X, op=ALU.max)

        def f_sub(c):
            nc.vector.tensor_tensor(out=grp(z[c]), in0=grp(q[c]), in1=spread(top[c][:]), op=ALU.subtract)
            nc.scalar.activation(e[c][:], z[c][:], ACT.Exp)

        def f_sum(c):
            nc.vector.tensor_reduce(out=sums[c][:], in_=grp(e[c]), axis=AX.X, op=ALU.add)

        def f_prod(c):
            nc.vector.tensor_tensor(out=prod[c][:], in0=halves(sums[c])[:, 0, :], in1=halves(sums[c])[:, 1, :], op=ALU.mult)

        def f_rec(c):
            nc.vector.reciprocal(out=rprod[c][:], in_=prod[c][:])

        def f_back(c):
            nc.vector.tensor_tensor(out=halves(rsum[c]), in0=halves(sums[c])[:, ::-1, :],
                                    in1=rprod[c][:].unsqueeze(1).to_broadcast([P, 2, V // 2]), op=ALU.mult)

        def f_mul(c):
            nc.vector.tensor_tensor(out=grp(price[c]), in0=grp(e[c]), in1=spread(rsum[c][:]), op=ALU.mult)

        def f_bel(c):
            cols = slice(c * W, (c + 1) * W)
            nc.vector.tensor_tensor(out=res[c][:], in0=price[c][:], in1=beliefs[:, cols], op=ALU.subtract)
            nc.sync.dma_start(out=out[:, cols], in_=res[c][:])

        stages = [f_q, f_max, f_sub, None, f_sum, f_prod, f_rec, f_back, f_mul, f_bel]
        lag = [0, 1, 3, 4]
        for step in range(len(stages) + lag[-1]):
            for c in reversed(range(CHUNKS)):
                if 0 <= step - lag[c] < len(stages) and stages[step - lag[c]] is not None:
                    stages[step - lag[c]](c)
